import numpy as np
import ml_dtypes


def mxq(x, axis, fmt="e4m3"):
    dtype, down = {"e4m3": (ml_dtypes.float8_e4m3fn, 7), "e5m2": (ml_dtypes.float8_e5m2, 14)}[fmt]
    v = np.moveaxis(np.asarray(x, np.float32).astype(ml_dtypes.bfloat16).astype(np.float64), axis, -1)
    blocks = v.reshape(v.shape[:-1] + (-1, 32))
    amax = np.abs(blocks).max(-1, keepdims=True)
    byte = np.maximum(np.where(amax > 0, np.frexp(amax)[1] - 1 + 127, 0) - down, 1)
    scale = np.exp2(byte - 127.0)
    codes = (blocks / scale).astype(np.float32).astype(dtype).astype(np.float64)
    return np.moveaxis((codes * scale).reshape(v.shape), -1, axis)


WIDE = False


def mx_kscale(k):
    if not WIDE:
        return np.ones(k)
    levels = np.array([10, -10, 5, -5, 0])
    if k % 512:
        return np.exp2(np.random.permutation(np.resize(levels, k // 32))).repeat(32)
    a = np.empty((k // 512, 16))
    for p in range(k // 512):
        a[p, :8] = np.random.permutation(np.resize(levels, 8))
        for g in range(8):
            far = levels[np.abs(levels - a[p, g]) >= 10]
            a[p, g + 8] = far[np.random.randint(len(far))]
    return np.exp2(a.ravel()).repeat(32)


def f64(x):
    return np.asarray(x).astype(np.float64)


def striped(idx):
    return np.tile(idx.reshape(-1, 16).T, (8, 1)).astype(np.uint16)


def unstriped(offs):
    return offs[:16].T.reshape(-1).astype(np.int64)


E2M1 = np.array([0.0, 0.5, 1.0, 1.5, 2.0, 3.0, 4.0, 6.0, -0.0, -0.5, -1.0, -1.5, -2.0, -3.0, -4.0, -6.0])


def pack_weight(w, fmt):
    k, n = w.shape
    w = f64(np.asarray(w, np.float32).astype(ml_dtypes.bfloat16)).reshape(k // 32, 32, n)
    amax = np.abs(w).max(1)
    if fmt == "e4m3":
        byte = np.frexp(amax)[1] - 1 + 127 - 7
    else:
        mant, ex = np.frexp(amax / 6.0)
        byte = np.where(mant > 0.5, ex, ex - 1) + 127
    byte = np.clip(np.where(amax > 0, byte, 1), 1, 254)
    scaled = (w * np.exp2(127.0 - byte)[:, None, :]).reshape(k, n).astype(np.float32)
    by_word = np.ascontiguousarray(scaled.reshape(k // 512, 128, 4, n).transpose(0, 1, 3, 2))
    if fmt == "e4m3":
        words = by_word.astype(ml_dtypes.float8_e4m3fn).view(np.uint8)
    else:
        c = by_word.astype(ml_dtypes.float4_e2m1fn).view(np.uint8) & 0xF
        words = (c[..., 0::2] | (c[..., 1::2] << 4)).reshape(k // 512, 128, 2 * n)
    return np.ascontiguousarray(words), np.ascontiguousarray(byte.astype(np.uint8).reshape(k // 512, 16, n))


def unpack_weight(words, scales, fmt):
    g, _, n = scales.shape
    words = np.ascontiguousarray(words).reshape(g, 128, n, -1)
    if fmt == "e4m3":
        vals = words.view(ml_dtypes.float8_e4m3fn).astype(np.float64)
    else:
        nib = np.empty((g, 128, n, 4), np.uint8)
        nib[..., 0::2] = words & 0xF
        nib[..., 1::2] = words >> 4
        vals = E2M1[nib]
    vals = vals * np.repeat(np.exp2(scales.astype(np.float64) - 127.0), 8, axis=1)[..., None]
    return vals.transpose(0, 1, 3, 2).reshape(g * 512, n)


def gelu(v):
    return 0.5 * v * (1.0 + np.tanh(np.sqrt(2.0 / np.pi) * (v + 0.044715 * v**3)))


K, T, S, P, H, M, N = 1536, 4096, 1024, 512, 1024, 512, 512


def setup_inputs():
    n = np.random.standard_normal
    s = mx_kscale(K)[:, None]
    u = mx_kscale(H)[:, None]
    q = mx_kscale(M)[:, None]
    d = {}
    d["tab_words"], d["tab_scales"] = pack_weight(n((K, T)) * s, "e2m1")
    d["offs"] = striped(np.random.permutation(T)[:S])
    d["pos1"] = striped(np.random.permutation(S)[:P])
    d["pos2"] = striped(np.random.permutation(S)[:P])
    d["w1"] = (0.7 * n((K, H)) / K**0.5 / s).astype(np.float32)
    d["gain"] = (np.exp(0.3 * n(H)) * u[:, 0]).astype(np.float32)
    d["w2_words"], d["w2_scales"] = pack_weight(0.9 * n((H, N)) / H**0.5 / u, "e2m1")
    d["ride"] = (n((M, P)) * q).astype(np.float32)
    d["w3"] = (1.2 * n((M, N)) / M**0.5 / q).astype(np.float32)
    d["base"] = (0.2 * np.exp(0.3 * n(N))).astype(np.float32)
    return d


def reference(tab_words, tab_scales, offs, pos1, pos2, w1, gain, w2_words, w2_scales, ride, w3, base):
    v = unpack_weight(tab_words, tab_scales, "e2m1")[:, unstriped(offs)]
    h = mxq(f64(w1), 0, "e4m3").T @ v
    diff = h[:, unstriped(pos1)] - h[:, unstriped(pos2)]
    z = np.square(diff) * f64(gain)[:, None]
    zq = mxq(z, 0, "e4m3")
    w2 = unpack_weight(w2_words, w2_scales, "e2m1")
    rq = mxq(f64(ride), 0, "e4m3")
    y = w2.T @ zq + mxq(f64(w3), 0, "e4m3").T @ rq
    return np.sqrt(np.abs(y) + f64(base)[:, None])

@@ -1,0 +1,287 @@
+from contextlib import ExitStack
+
+import concourse.mybir as mybir
+
+K, T, S, PAIRS, H, M, N = 1536, 4096, 1024, 512, 1024, 512, 512
+FLOPS = 2 * K * H * S + 2 * H * N * PAIRS + 2 * M * N * PAIRS
+
+F32 = mybir.dt.float32
+BF16 = mybir.dt.bfloat16
+I32 = mybir.dt.int32
+U32 = mybir.dt.uint32
+U16 = mybir.dt.uint16
+U8 = mybir.dt.uint8
+FP8X4 = mybir.dt.float8_e4m3fn_x4
+FP4X4 = mybir.dt.float4_e2m1fn_x4
+ALU = mybir.AluOpType
+ACT = mybir.ActivationFunctionType
+
+P = 128
+PACK = 4
+K_PASS = P * PACK
+BANK = 512
+K_PASSES = K // K_PASS
+H_PASSES = H // K_PASS
+N_TILES = N // P
+LIST_COL = 16
+MOVED_ROWS = 112
+LAST_CHUNKS = (256, 128, 128)
+
+
+def tile_list_carrier_mismatch_scores_kernel(
+    tc, tab_words, tab_scales, offs, pos1, pos2, w1, gain, w2_words, w2_scales, ride, w3, base, out
+):
+    nc = tc.nc
+    with ExitStack() as ctx:
+        held = ctx.enter_context(tc.tile_pool(name="held", bufs=1))
+        psum = ctx.enter_context(tc.psum_pool(name="psum", bufs=1))
+
+        def tile(shape, dtype, name, **kw):
+            return held.tile(shape, dtype, name=name, align_bytes=64, **kw)
+
+        table_scales = tile([P, T], U8, "table_scales", tag="table_scales")
+        nc.vector.memset(table_scales[:].bitcast(I32), 0)
+        picked_scales = [tile([P, S], U8, "picked_scales%d" % a) for a in range(K_PASSES)]
+        for a in range(1, K_PASSES):
+            nc.vector.memset(picked_scales[a][:].bitcast(I32), 0)
+        w2_scale_t = tile([P, H_PASSES, N], U8, "w2_scale_t")
+        nc.vector.memset(w2_scale_t[:].bitcast(I32), 0)
+        one = tile([P, 1], F32, "one")
+        nc.vector.memset(one[:], 1.0)
+        warm = tile([P, 1], F32, "warm")
+        nc.scalar.activation(warm[:], one[:], ACT.Sqrt)
+
+        offs_t = tile([P, S // LIST_COL], U16, "offs_t")
+        pos1_t = tile([P, PAIRS // LIST_COL], U16, "pos1_t")
+        pos2_t = tile([P, PAIRS // LIST_COL], U16, "pos2_t")
+        table_words = [tile([P, T], U16, "table_words%d" % a) for a in range(K_PASSES)]
+        gain_t = tile([P, H_PASSES, PACK], F32, "gain_t")
+        base_t = tile([P, N_TILES], F32, "base_t")
+
+        def load_words(a):
+            nc.sync.dma_start(table_words[a][:].bitcast(I32), tab_words[a].bitcast(I32))
+
+        w1_raw = {}
+
+        def load_w1(b, a, part, parts):
+            width = K_PASS // parts
+            name = "w1_raw_%d_%d_%d" % (b, a, part)
+            raw = tile([P, PACK, width], F32, name, tag=name)
+            c0 = b * K_PASS + part * width
+            rows = w1[a * K_PASS : (a + 1) * K_PASS, c0 : c0 + width]
+            nc.sync.dma_start(raw[:], rows.rearrange("(p j) c -> p j c", j=PACK))
+            w1_raw[b, a, part] = raw
+
+        nc.sync.dma_start(offs_t[:], offs)
+        load_words(0)
+        for q in range(4):
+            nc.gpsimd.dma_start(
+                table_scales[32 * q : 32 * q + 4 * K_PASSES, :].bitcast(I32),
+                tab_scales[:, 4 * q : 4 * q + 4, :].bitcast(I32),
+            )
+        load_w1(0, 0, 0, 1)
+        load_words(1)
+        load_words(2)
+        for a in (1, 2):
+            for part in range(2):
+                load_w1(0, a, part, 2)
+        nc.sync.dma_start(pos1_t[:], pos1)
+        nc.sync.dma_start(pos2_t[:], pos2)
+        nc.sync.dma_start(gain_t[:], gain.rearrange("(b p t) -> p b t", b=H_PASSES, t=PACK))
+        for a in range(K_PASSES):
+            load_w1(1, a, 0, 1)
+        ride_raw = tile([P, PACK, PAIRS], F32, "ride_raw")
+        nc.sync.dma_start(ride_raw[:], ride.rearrange("(p j) c -> p j c", j=PACK))
+        w3_raw = tile([P, PACK, N], F32, "w3_raw")
+        nc.sync.dma_start(w3_raw[:], w3.rearrange("(p j) c -> p j c", j=PACK))
+        w2_word_t = tile([P, H_PASSES, 2 * N], U8, "w2_word_t")
+        nc.sync.dma_start(w2_word_t[:].bitcast(I32), w2_words.rearrange("a p n -> p a n").bitcast(I32))
+        for q in range(4):
+            nc.sync.dma_start(
+                w2_scale_t[32 * q : 32 * q + 4].bitcast(I32),
+                w2_scales[:, 4 * q : 4 * q + 4, :].rearrange("a r n -> r a n").bitcast(I32),
+            )
+
+        with nc.allow_non_contiguous_dma(reason="one value a partition"):
+            nc.sync.dma_start(base_t[:], base.rearrange("(u p) -> p u", p=P))
+
+        picked_words = {}
+        w1_grouped, w1_codes, w1_scales = {}, {}, {}
+
+        def gather_words(a):
+            picked_words[a] = tile([P, S], U16, "picked_words", tag="table_scales" if a == 1 else "picked_words%d" % a)
+            nc.vector.tensor_copy(picked_words[a][:], table_words[a][:].indirect(offs_t[:]))
+
+        def group_w1(b, a, part, parts, engine_copy):
+            if part == 0:
+                w1_grouped[b, a] = tile([P, PACK, P, PACK], BF16, "w1_grouped", tag="w1_grouped_%d_%d" % (b, a))
+            span = P // parts
+            dst = w1_grouped[b, a][:, :, part * span : (part + 1) * span, :].rearrange("p t m j -> p m j t")
+            src = w1_raw[b, a, part][:].rearrange("p j (m t) -> p m j t", t=PACK)
+            engine_copy(dst, src)
+
+        def quantize_w1(b, a, pieces):
+            codes = tile([P, K_PASS], U32, "w1_codes_%d_%d" % (b, a))
+            scales = tile([P, K_PASS], U8, "w1_scales_%d_%d" % (b, a))
+            flat = w1_grouped[b, a][:].rearrange("p t m j -> p (t m j)")
+            step = K_PASS // pieces
+            for i in range(pieces):
+                nc.vector.quantize_mx(
+                    out=codes[:, i * step : (i + 1) * step].bitcast(FP8X4),
+                    scales=scales[:, i * step : (i + 1) * step],
+                    in_=flat[:, PACK * i * step : PACK * (i + 1) * step],
+                )
+            w1_codes[b, a], w1_scales[b, a] = codes, scales
+
+        gather_words(0)
+        nc.vector.tensor_copy(picked_scales[0][:], table_scales[:].indirect(offs_t[:]))
+        for a in range(1, K_PASSES):
+            nc.scalar.dma_start(
+                picked_scales[a][0:MOVED_ROWS, :].bitcast(I32),
+                picked_scales[0][4 * a : 4 * a + MOVED_ROWS, :].bitcast(I32),
+            )
+        group_w1(0, 0, 0, 1, nc.scalar.copy)
+        gather_words(1)
+        gather_words(2)
+        quantize_w1(0, 0, 1)
+        group_w1(0, 1, 0, 2, nc.scalar.copy)
+        group_w1(0, 1, 1, 2, nc.scalar.copy)
+        quantize_w1(0, 1, 1)
+        group_w1(0, 2, 0, 2, nc.scalar.copy)
+        group_w1(0, 2, 1, 2, nc.vector.tensor_copy)
+        quantize_w1(0, 2, 4)
+
+        h_rows = {}
+        halves = [slice(i * BANK, (i + 1) * BANK) for i in range(S // BANK)]
+
+        def features(b):
+            banks = [psum.tile([P, BANK], F32, name="h_bank", tag="bank%d" % i) for i in range(8)]
+            for a in range(K_PASSES):
+                for t in range(PACK):
+                    cols = slice(t * P, (t + 1) * P)
+                    for i, js in enumerate(halves):
+                        nc.tensor.matmul_mx(
+                            out=banks[2 * t + i][:],
+                            lhsT=w1_codes[b, a][:, cols].bitcast(FP8X4),
+                            lhsT_scale=w1_scales[b, a][:, cols],
+                            rhs=picked_words[a][:, js].bitcast(FP4X4),
+                            rhs_scale=picked_scales[a][:, js],
+                            start=(a == 0),
+                            stop=(a == K_PASSES - 1),
+                        )
+            for t in range(PACK):
+                h_rows[b, t] = tile([P, S], F32, "h_%d_%d" % (b, t))
+                for i, js in enumerate(halves):
+                    copy = nc.vector.tensor_copy if (b, t, i) == (0, 0, 1) else nc.scalar.copy
+                    copy(h_rows[b, t][:, js], banks[2 * t + i][:])
+
+        z_rows = [tile([P, PACK, PAIRS], BF16, "z_rows%d" % b) for b in range(H_PASSES)]
+
+        def mismatch(b, units, left_tag=None, diff_tag=None):
+            width = units[0][2]
+            shape = [P, len(units), width]
+            left = tile(shape, F32, "left", tag=left_tag) if left_tag else tile(shape, F32, "left", tag="left", bufs=2)
+            diff = tile(shape, F32, "diff", tag=diff_tag) if diff_tag else tile(shape, F32, "diff", tag="diff", bufs=2)
+            lists = [slice(j0 // LIST_COL, (j0 + width) // LIST_COL) for t, j0, w in units]
+            for i, (t, j0, w) in enumerate(units):
+                nc.vector.tensor_copy(left[:, i, :], h_rows[b, t][:].indirect(pos1_t[:, lists[i]]))
+            for i, (t, j0, w) in enumerate(units):
+                nc.vector.tensor_tensor(
+                    diff[:, i, :], h_rows[b, t][:].indirect(pos2_t[:, lists[i]]), left[:, i, :], ALU.subtract
+                )
+            for i, (t, j0, w) in enumerate(units):
+                nc.vector.scalar_tensor_tensor(
+                    z_rows[b][:, t, j0 : j0 + width], diff[:, i, :], gain_t[:, b, t : t + 1], diff[:, i, :], ALU.mult, ALU.mult
+                )
+
+        def group(rows, width, name, engine_copy):
+            grouped = tile([P, width, PACK], BF16, name + "_grouped", tag=name + "_grouped")
+            engine_copy(
+                grouped[:].rearrange("p (c i) t -> p c t i", i=PACK),
+                rows.rearrange("p t (c i) -> p c t i", i=PACK),
+            )
+            return grouped
+
+        def quantize(grouped, width, name):
+            codes = tile([P, width], U32, name + "_codes")
+            scales = tile([P, width], U8, name + "_scales")
+            nc.vector.quantize_mx(
+                out=codes[:].bitcast(FP8X4), scales=scales[:], in_=grouped[:].rearrange("p c t -> p (c t)")
+            )
+            return codes, scales
+
+        def in_two(t, j0, width):
+            return [(t, j0, width // 2), (t, j0 + width // 2, width // 2)]
+
+        features(0)
+        for a in range(K_PASSES):
+            group_w1(1, a, 0, 1, nc.scalar.copy)
+        mismatch(0, in_two(0, 0, PAIRS))
+        mismatch(0, in_two(1, 0, PAIRS))
+        quantize_w1(1, 0, 1)
+        mismatch(0, in_two(2, 0, PAIRS), left_tag="w1_grouped_1_0")
+        quantize_w1(1, 1, 1)
+        quantize_w1(1, 2, 1)
+        features(1)
+        mismatch(0, in_two(3, 0, PAIRS), left_tag="w1_grouped_1_1", diff_tag="w1_grouped_1_2")
+        ride_codes, ride_scales = quantize(group(ride_raw[:], PAIRS, "ride", nc.scalar.copy), PAIRS, "ride")
+        w3_grouped = group(w3_raw[:], N, "w3", nc.scalar.copy)
+        z0_grouped = group(z_rows[0][:], PAIRS, "z0", nc.scalar.copy)
+
+        y_banks = [psum.tile([P, N_TILES, P], F32, name="y_bank", tag="bank%d" % c) for c in range(PAIRS // P)]
+        spare = ["w1_raw_1_0_0", "w1_raw_1_1_0", "w1_raw_1_2_0", "w1_raw_0_0_0", "w1_raw_0_1_0", "w1_raw_0_1_1"]
+
+        def w3_pass(c):
+            for u in range(N_TILES):
+                nc.tensor.matmul_mx(
+                    out=y_banks[c][:, u, :],
+                    lhsT=w3_codes[:, P * u : P * (u + 1)].bitcast(FP8X4),
+                    lhsT_scale=w3_scales[:, P * u : P * (u + 1)],
+                    rhs=ride_codes[:, c * P : (c + 1) * P].bitcast(FP8X4),
+                    rhs_scale=ride_scales[:, c * P : (c + 1) * P],
+                    start=(u == 0),
+                    stop=False,
+                )
+
+        def w2_pass(c, b, codes, scales, i):
+            for u in range(N_TILES):
+                nc.tensor.matmul_mx(
+                    out=y_banks[c][:, u, :],
+                    lhsT=w2_word_t[:, b, 2 * P * u : 2 * P * (u + 1)].bitcast(FP4X4),
+                    lhsT_scale=w2_scale_t[:, b, P * u : P * (u + 1)],
+                    rhs=codes[:, i * P : (i + 1) * P].bitcast(FP8X4),
+                    rhs_scale=scales[:, i * P : (i + 1) * P],
+                    start=False,
+                    stop=(b == H_PASSES - 1 and u == N_TILES - 1),
+                )
+
+        def finish(j0, width, codes, scales):
+            size = tile([P, N_TILES, width], F32, "size", tag=spare.pop())
+            score = tile([P, N_TILES, width], F32, "score", tag=spare.pop())
+            for i in range(width // P):
+                w2_pass(j0 // P + i, 1, codes, scales, i)
+                nc.scalar.activation(size[:, :, i * P : (i + 1) * P], y_banks[j0 // P + i][:], ACT.Abs)
+            for u in range(N_TILES):
+                nc.scalar.activation(score[:, u, :], size[:, u, :], ACT.Sqrt, bias=base_t[:, u : u + 1])
+            nc.sync.dma_start(out[:, j0 : j0 + width].rearrange("(u p) j -> p u j", p=P), score[:])
+
+        for t in range(PACK):
+            mismatch(1, in_two(t, 0, 256))
+        w3_codes, w3_scales = quantize(w3_grouped, N, "w3")
+        for c in range(PAIRS // P):
+            w3_pass(c)
+        za_grouped = group(z_rows[1][:, :, 0:256], 256, "za", nc.scalar.copy)
+        mismatch(1, [(0, 256, 128), (1, 256, 128)], left_tag="w3_grouped")
+        z0_codes, z0_scales = quantize(z0_grouped, PAIRS, "z0")
+        za_codes, za_scales = quantize(za_grouped, 256, "za")
+        for c in range(PAIRS // P):
+            w2_pass(c, 0, z0_codes, z0_scales, c)
+        mismatch(1, [(2, 256, 128), (3, 256, 128)], left_tag="z0_grouped", diff_tag="za_grouped")
+        zb_grouped = group(z_rows[1][:, :, 256:384], 128, "zb", nc.scalar.copy)
+        finish(0, 256, za_codes, za_scales)
+        mismatch(1, [(0, 384, 128), (1, 384, 128)])
+        zb_codes, zb_scales = quantize(zb_grouped, 128, "zb")
+        mismatch(1, [(2, 384, 128), (3, 384, 128)], left_tag="zb_grouped")
+        finish(256, 128, zb_codes, zb_scales)
+        zc_codes, zc_scales = quantize(group(z_rows[1][:, :, 384:512], 128, "zc", nc.vector.tensor_copy), 128, "zc")
+        finish(384, 128, zc_codes, zc_scales)

@@ -24,7 +24,7 @@ K_PASSES = K // K_PASS
 H_PASSES = H // K_PASS
 N_TILES = N // P
 LIST_COL = 16
-MOVED_ROWS = 112
+SCALE_ROW = (32, 48, 112)
 LAST_CHUNKS = (256, 128, 128)
 
 
@@ -39,163 +39,80 @@ def tile_list_carrier_mismatch_scores_kernel(
         def tile(shape, dtype, name, **kw):
             return held.tile(shape, dtype, name=name, align_bytes=64, **kw)
 
-        table_scales = tile([P, T], U8, "table_scales", tag="table_scales")
-        nc.vector.memset(table_scales[:].bitcast(I32), 0)
+        table_scales = tile([P, T], U8, "table_scales", tag="stage_a")
+        nc.vector.memset(table_scales[0:32, :].bitcast(I32), 0)
+        nc.gpsimd.memset(table_scales[64:112, :].bitcast(I32), 0)
+        gathered_scales = tile([P, S], U8, "gathered_scales")
         picked_scales = [tile([P, S], U8, "picked_scales%d" % a) for a in range(K_PASSES)]
-        for a in range(1, K_PASSES):
-            nc.vector.memset(picked_scales[a][:].bitcast(I32), 0)
-        w2_scale_t = tile([P, H_PASSES, N], U8, "w2_scale_t")
-        nc.vector.memset(w2_scale_t[:].bitcast(I32), 0)
         one = tile([P, 1], F32, "one")
         nc.vector.memset(one[:], 1.0)
+        for a in range(K_PASSES):
+            nc.vector.memset(picked_scales[a][:].bitcast(I32), 0)
+        w2_scale_t = tile([P, H_PASSES, N], U8, "w2_scale_t")
+        nc.gpsimd.memset(w2_scale_t[:].bitcast(I32), 0)
         warm = tile([P, 1], F32, "warm")
         nc.scalar.activation(warm[:], one[:], ACT.Sqrt)
 
         offs_t = tile([P, S // LIST_COL], U16, "offs_t")
         pos1_t = tile([P, PAIRS // LIST_COL], U16, "pos1_t")
         pos2_t = tile([P, PAIRS // LIST_COL], U16, "pos2_t")
-        table_words = [tile([P, T], U16, "table_words%d" % a) for a in range(K_PASSES)]
-        gain_t = tile([P, H_PASSES, PACK], F32, "gain_t")
+        gain_t = [tile([P, PACK], F32, "gain_t%d" % b) for b in range(H_PASSES)]
         base_t = tile([P, N_TILES], F32, "base_t")
+        table_words, w1_raw = {}, {}
 
-        def load_words(a):
+        def load_words(a, stage):
+            table_words[a] = tile([P, T], U16, "table_words", tag=stage)
             nc.sync.dma_start(table_words[a][:].bitcast(I32), tab_words[a].bitcast(I32))
 
-        w1_raw = {}
-
-        def load_w1(b, a, part, parts):
-            width = K_PASS // parts
-            name = "w1_raw_%d_%d_%d" % (b, a, part)
-            raw = tile([P, PACK, width], F32, name, tag=name)
-            c0 = b * K_PASS + part * width
-            rows = w1[a * K_PASS : (a + 1) * K_PASS, c0 : c0 + width]
+        def load_rows(rows, stage):
+            raw = tile([P, PACK, rows.shape[1]], F32, "raw", tag=stage)
             nc.sync.dma_start(raw[:], rows.rearrange("(p j) c -> p j c", j=PACK))
-            w1_raw[b, a, part] = raw
+            return raw
 
+        def load_w1(b, a, part, stage):
+            width = K_PASS // 2 if b == 0 else K_PASS
+            c0 = b * K_PASS + part * width
+            w1_raw[b, a, part] = load_rows(w1[a * K_PASS : (a + 1) * K_PASS, c0 : c0 + width], stage)
+
+        scale_rows = tab_scales.rearrange("a q t -> (a q) t")
         nc.sync.dma_start(offs_t[:], offs)
-        load_words(0)
-        for q in range(4):
-            nc.gpsimd.dma_start(
-                table_scales[32 * q : 32 * q + 4 * K_PASSES, :].bitcast(I32),
-                tab_scales[:, 4 * q : 4 * q + 4, :].bitcast(I32),
-            )
-        load_w1(0, 0, 0, 1)
-        load_words(1)
-        load_words(2)
-        for a in (1, 2):
-            for part in range(2):
-                load_w1(0, a, part, 2)
+        nc.sync.dma_start(table_scales[32:64, :].bitcast(I32), scale_rows[0:32, :].bitcast(I32))
+        nc.sync.dma_start(table_scales[112:128, :].bitcast(I32), scale_rows[32:48, :].bitcast(I32))
+        load_words(0, "stage_b")
         nc.sync.dma_start(pos1_t[:], pos1)
         nc.sync.dma_start(pos2_t[:], pos2)
-        nc.sync.dma_start(gain_t[:], gain.rearrange("(b p t) -> p b t", b=H_PASSES, t=PACK))
-        for a in range(K_PASSES):
-            load_w1(1, a, 0, 1)
-        ride_raw = tile([P, PACK, PAIRS], F32, "ride_raw")
-        nc.sync.dma_start(ride_raw[:], ride.rearrange("(p j) c -> p j c", j=PACK))
-        w3_raw = tile([P, PACK, N], F32, "w3_raw")
-        nc.sync.dma_start(w3_raw[:], w3.rearrange("(p j) c -> p j c", j=PACK))
+        load_words(1, "stage_c")
+        load_w1(0, 0, 0, "stage_d")
+        with nc.allow_non_contiguous_dma(reason="one value a partition"):
+            nc.gpsimd.dma_start(gain_t[0][:], gain[0:K_PASS].rearrange("(m p) -> p m", p=P))
+        nc.gpsimd.dma_start(gain_t[1][:], gain[K_PASS:H].rearrange("(p t) -> p t", t=PACK))
         w2_word_t = tile([P, H_PASSES, 2 * N], U8, "w2_word_t")
-        nc.sync.dma_start(w2_word_t[:].bitcast(I32), w2_words.rearrange("a p n -> p a n").bitcast(I32))
+        nc.gpsimd.dma_start(w2_word_t[:].bitcast(I32), w2_words.rearrange("a p n -> p a n").bitcast(I32))
         for q in range(4):
-            nc.sync.dma_start(
+            nc.gpsimd.dma_start(
                 w2_scale_t[32 * q : 32 * q + 4].bitcast(I32),
                 w2_scales[:, 4 * q : 4 * q + 4, :].rearrange("a r n -> r a n").bitcast(I32),
             )
-
         with nc.allow_non_contiguous_dma(reason="one value a partition"):
-            nc.sync.dma_start(base_t[:], base.rearrange("(u p) -> p u", p=P))
+            nc.gpsimd.dma_start(base_t[:], base.rearrange("(u p) -> p u", p=P))
 
-        picked_words = {}
-        w1_grouped, w1_codes, w1_scales = {}, {}, {}
+        picked_words = [tile([P, S], U16, "picked_words%d" % a) for a in range(K_PASSES)]
+        w1_grouped, w1_mx = {}, {}
 
         def gather_words(a):
-            picked_words[a] = tile([P, S], U16, "picked_words", tag="table_scales" if a == 1 else "picked_words%d" % a)
             nc.vector.tensor_copy(picked_words[a][:], table_words[a][:].indirect(offs_t[:]))
 
-        def group_w1(b, a, part, parts, engine_copy):
-            if part == 0:
-                w1_grouped[b, a] = tile([P, PACK, P, PACK], BF16, "w1_grouped", tag="w1_grouped_%d_%d" % (b, a))
-            span = P // parts
-            dst = w1_grouped[b, a][:, :, part * span : (part + 1) * span, :].rearrange("p t m j -> p m j t")
-            src = w1_raw[b, a, part][:].rearrange("p j (m t) -> p m j t", t=PACK)
-            engine_copy(dst, src)
-
-        def quantize_w1(b, a, pieces):
-            codes = tile([P, K_PASS], U32, "w1_codes_%d_%d" % (b, a))
-            scales = tile([P, K_PASS], U8, "w1_scales_%d_%d" % (b, a))
-            flat = w1_grouped[b, a][:].rearrange("p t m j -> p (t m j)")
-            step = K_PASS // pieces
-            for i in range(pieces):
-                nc.vector.quantize_mx(
-                    out=codes[:, i * step : (i + 1) * step].bitcast(FP8X4),
-                    scales=scales[:, i * step : (i + 1) * step],
-                    in_=flat[:, PACK * i * step : PACK * (i + 1) * step],
-                )
-            w1_codes[b, a], w1_scales[b, a] = codes, scales
-
-        gather_words(0)
-        nc.vector.tensor_copy(picked_scales[0][:], table_scales[:].indirect(offs_t[:]))
-        for a in range(1, K_PASSES):
-            nc.scalar.dma_start(
-                picked_scales[a][0:MOVED_ROWS, :].bitcast(I32),
-                picked_scales[0][4 * a : 4 * a + MOVED_ROWS, :].bitcast(I32),
-            )
-        group_w1(0, 0, 0, 1, nc.scalar.copy)
-        gather_words(1)
-        gather_words(2)
-        quantize_w1(0, 0, 1)
-        group_w1(0, 1, 0, 2, nc.scalar.copy)
-        group_w1(0, 1, 1, 2, nc.scalar.copy)
-        quantize_w1(0, 1, 1)
-        group_w1(0, 2, 0, 2, nc.scalar.copy)
-        group_w1(0, 2, 1, 2, nc.vector.tensor_copy)
-        quantize_w1(0, 2, 4)
-
-        h_rows = {}
-        halves = [slice(i * BANK, (i + 1) * BANK) for i in range(S // BANK)]
-
-        def features(b):
-            banks = [psum.tile([P, BANK], F32, name="h_bank", tag="bank%d" % i) for i in range(8)]
-            for a in range(K_PASSES):
-                for t in range(PACK):
-                    cols = slice(t * P, (t + 1) * P)
-                    for i, js in enumerate(halves):
-                        nc.tensor.matmul_mx(
-                            out=banks[2 * t + i][:],
-                            lhsT=w1_codes[b, a][:, cols].bitcast(FP8X4),
-                            lhsT_scale=w1_scales[b, a][:, cols],
-                            rhs=picked_words[a][:, js].bitcast(FP4X4),
-                            rhs_scale=picked_scales[a][:, js],
-                            start=(a == 0),
-                            stop=(a == K_PASSES - 1),
-                        )
-            for t in range(PACK):
-                h_rows[b, t] = tile([P, S], F32, "h_%d_%d" % (b, t))
-                for i, js in enumerate(halves):
-                    copy = nc.vector.tensor_copy if (b, t, i) == (0, 0, 1) else nc.scalar.copy
-                    copy(h_rows[b, t][:, js], banks[2 * t + i][:])
-
-        z_rows = [tile([P, PACK, PAIRS], BF16, "z_rows%d" % b) for b in range(H_PASSES)]
-
-        def mismatch(b, units, left_tag=None, diff_tag=None):
-            width = units[0][2]
-            shape = [P, len(units), width]
-            left = tile(shape, F32, "left", tag=left_tag) if left_tag else tile(shape, F32, "left", tag="left", bufs=2)
-            diff = tile(shape, F32, "diff", tag=diff_tag) if diff_tag else tile(shape, F32, "diff", tag="diff", bufs=2)
-            lists = [slice(j0 // LIST_COL, (j0 + width) // LIST_COL) for t, j0, w in units]
-            for i, (t, j0, w) in enumerate(units):
-                nc.vector.tensor_copy(left[:, i, :], h_rows[b, t][:].indirect(pos1_t[:, lists[i]]))
-            for i, (t, j0, w) in enumerate(units):
-                nc.vector.tensor_tensor(
-                    diff[:, i, :], h_rows[b, t][:].indirect(pos2_t[:, lists[i]]), left[:, i, :], ALU.subtract
-                )
-            for i, (t, j0, w) in enumerate(units):
-                nc.vector.scalar_tensor_tensor(
-                    z_rows[b][:, t, j0 : j0 + width], diff[:, i, :], gain_t[:, b, t : t + 1], diff[:, i, :], ALU.mult, ALU.mult
+        def place_scales(a):
+            first = SCALE_ROW[a]
+            for q in range(4):
+                nc.sync.dma_start(
+                    picked_scales[a][32 * q : 32 * q + 4, :].bitcast(I32),
+                    gathered_scales[first + 4 * q : first + 4 * q + 4, :].bitcast(I32),
                 )
 
-        def group(rows, width, name, engine_copy):
-            grouped = tile([P, width, PACK], BF16, name + "_grouped", tag=name + "_grouped")
+        def group(rows, width, name, engine_copy, grouped=None):
+            if grouped is None:
+                grouped = tile([P, width, PACK], BF16, name + "_grouped", tag=name + "_grouped")
             engine_copy(
                 grouped[:].rearrange("p (c i) t -> p c t i", i=PACK),
                 rows.rearrange("p t (c i) -> p c t i", i=PACK),
@@ -203,33 +120,142 @@ def tile_list_carrier_mismatch_scores_kernel(
             return grouped
 
         def quantize(grouped, width, name):
-            codes = tile([P, width], U32, name + "_codes")
-            scales = tile([P, width], U8, name + "_scales")
+            codes = tile([P, width], U32, name + "_codes", tag=name + "_codes")
+            scales = tile([P, width], U8, name + "_scales", tag=name + "_scales")
             nc.vector.quantize_mx(
                 out=codes[:].bitcast(FP8X4), scales=scales[:], in_=grouped[:].rearrange("p c t -> p (c t)")
             )
             return codes, scales
 
+        def group_w1(b, a, part):
+            name = "w1_%d_%d_%d" % (b, a, part)
+            if b == 0:
+                w1_grouped[b, a, part] = group(w1_raw[b, a, part][:], K_PASS // 2, name, nc.scalar.copy)
+            else:
+                grouped = tile([P, K_PASS, PACK], BF16, name + "_grouped", tag=name + "_grouped")
+                nc.scalar.copy(
+                    grouped[:].rearrange("p (t m) j -> p m j t", t=PACK),
+                    w1_raw[b, a, part][:].rearrange("p j (m t) -> p m j t", t=PACK),
+                )
+                w1_grouped[b, a, part] = grouped
+
+        def quantize_w1(b, a, part):
+            grouped = w1_grouped[b, a, part]
+            w1_mx[b, a, part] = quantize(grouped, grouped.shape[1], "w1_%d_%d_%d" % (b, a, part))
+
+        nc.vector.tensor_copy(gathered_scales[:], table_scales[:].indirect(offs_t[:]))
+        place_scales(0)
+        load_w1(0, 1, 0, "stage_a")
+        place_scales(1)
+        gather_words(0)
+        load_words(2, "stage_b")
+        group_w1(0, 0, 0)
+        load_w1(0, 2, 0, "stage_d")
+        place_scales(2)
+        gather_words(1)
+        load_w1(0, 0, 1, "stage_c")
+        quantize_w1(0, 0, 0)
+        group_w1(0, 1, 0)
+        load_w1(0, 1, 1, "stage_a")
+        quantize_w1(0, 1, 0)
+        gather_words(2)
+        load_w1(0, 2, 1, "stage_b")
+        group_w1(0, 2, 0)
+        load_w1(1, 0, 0, "stage_d")
+        quantize_w1(0, 2, 0)
+        load_w1(1, 1, 0, "w1_0_2_0_grouped")
+
+        halves = [slice(i * BANK, (i + 1) * BANK) for i in range(S // BANK)]
+        h_rows = {}
+
+        def features(b, part, slices):
+            banks = {}
+            for t in slices:
+                for i in range(2):
+                    banks[t, i] = psum.tile([P, BANK], F32, name="h_bank", tag="bank%d" % (2 * t + i))
+            for a in range(K_PASSES):
+                codes, scales = w1_mx[b, a, part]
+                for t in slices:
+                    cols = slice((t - slices[0]) * P, (t - slices[0] + 1) * P)
+                    for i, js in enumerate(halves):
+                        nc.tensor.matmul_mx(
+                            out=banks[t, i][:],
+                            lhsT=codes[:, cols].bitcast(FP8X4),
+                            lhsT_scale=scales[:, cols],
+                            rhs=picked_words[a][:, js].bitcast(FP4X4),
+                            rhs_scale=picked_scales[a][:, js],
+                            start=(a == 0),
+                            stop=(a == K_PASSES - 1),
+                        )
+            for t in slices:
+                h_rows[b, t] = tile([P, S], F32, "h_%d_%d" % (b, t))
+                for i, js in enumerate(halves):
+                    copy = nc.vector.tensor_copy if (b, t, i) == (0, 0, 1) else nc.scalar.copy
+                    copy(h_rows[b, t][:, js], banks[t, i][:])
+
+        z_rows = [tile([P, PACK, PAIRS], BF16, "z_rows%d" % b) for b in range(H_PASSES)]
+        z_plain = [tile([P, PAIRS], BF16, "z_plain%d" % m) for m in range(PACK)]
+
+        def mismatch(b, units, left_tag=None, diff_tag=None, on_scalar=False):
+            width = units[0][2]
+            shape = [P, len(units), width]
+            left = tile(shape, F32, "left", tag=left_tag) if left_tag else tile(shape, F32, "left", tag="left", bufs=2)
+            diff = tile(shape, F32, "diff", tag=diff_tag) if diff_tag else tile(shape, F32, "diff", tag="diff", bufs=4)
+            lists = [slice(j0 // LIST_COL, (j0 + width) // LIST_COL) for t, j0, w in units]
+            for i, (t, j0, w) in enumerate(units):
+                nc.vector.tensor_copy(left[:, i, :], h_rows[b, t][:].indirect(pos1_t[:, lists[i]]))
+            for i, (t, j0, w) in enumerate(units):
+                nc.vector.tensor_tensor(
+                    diff[:, i, :], h_rows[b, t][:].indirect(pos2_t[:, lists[i]]), left[:, i, :], ALU.subtract
+                )
+            if on_scalar:
+                t, j0 = units[0][0], units[0][1]
+                js = slice(j0, j0 + len(units) * width)
+                z = z_plain[t][:, js] if b == 0 else z_rows[b][:, t, js]
+                flat = diff[:].rearrange("p i w -> p (i w)")
+                nc.scalar.activation(flat, flat, ACT.Square)
+                nc.scalar.activation(z, flat, ACT.Copy, scale=gain_t[b][:, t : t + 1])
+                return
+            for i, (t, j0, w) in enumerate(units):
+                z = z_plain[t][:, j0 : j0 + width] if b == 0 else z_rows[b][:, t, j0 : j0 + width]
+                nc.vector.scalar_tensor_tensor(z, diff[:, i, :], gain_t[b][:, t : t + 1], diff[:, i, :], ALU.mult, ALU.mult)
+
         def in_two(t, j0, width):
             return [(t, j0, width // 2), (t, j0 + width // 2, width // 2)]
 
-        features(0)
+        def first_half_slice(m, **holds):
+            mismatch(0, in_two(m, 0, PAIRS), **holds)
+            nc.sync.dma_start(z_rows[0][32 * m : 32 * (m + 1)], z_plain[m][:])
+
+        features(0, 0, [0, 1])
+        part = K_PASS // 2
+        late_a = tile([P, part, PACK], BF16, "late_a", tag="w1_0_2_0_codes")
+        late_b = tile([P, 2 * part, PACK], BF16, "late_b", tag="w1_0_2_0_scales")
+        group(w1_raw[0, 0, 1][:], part, "", nc.scalar.copy, late_a)
+        load_w1(1, 2, 0, "stage_c")
+        group(w1_raw[0, 1, 1][:], part, "", nc.scalar.copy, late_b[:, 0:part, :])
+        ride_raw = load_rows(ride, "stage_a")
+        group(w1_raw[0, 2, 1][:], part, "", nc.scalar.copy, late_b[:, part : 2 * part, :])
+        w3_raw = load_rows(w3, "stage_b")
+        first_half_slice(0)
+        w1_mx[0, 0, 1] = quantize(late_a, part, "late_a")
+        codes, scales = quantize(late_b, 2 * part, "late_b")
+        for a in (1, 2):
+            w1_mx[0, a, 1] = codes[:, (a - 1) * part : a * part], scales[:, (a - 1) * part : a * part]
+        features(0, 1, [2, 3])
         for a in range(K_PASSES):
-            group_w1(1, a, 0, 1, nc.scalar.copy)
-        mismatch(0, in_two(0, 0, PAIRS))
-        mismatch(0, in_two(1, 0, PAIRS))
-        quantize_w1(1, 0, 1)
-        mismatch(0, in_two(2, 0, PAIRS), left_tag="w1_grouped_1_0")
-        quantize_w1(1, 1, 1)
-        quantize_w1(1, 2, 1)
-        features(1)
-        mismatch(0, in_two(3, 0, PAIRS), left_tag="w1_grouped_1_1", diff_tag="w1_grouped_1_2")
+            group_w1(1, a, 0)
+        first_half_slice(1, left_tag="w1_0_2_0_codes", diff_tag="w1_0_2_0_scales")
+        first_half_slice(2)
+        for a in range(K_PASSES):
+            quantize_w1(1, a, 0)
+        features(1, 0, [0, 1, 2, 3])
+        first_half_slice(3, left_tag="w1_1_1_0_grouped", diff_tag="w1_1_2_0_grouped")
         ride_codes, ride_scales = quantize(group(ride_raw[:], PAIRS, "ride", nc.scalar.copy), PAIRS, "ride")
-        w3_grouped = group(w3_raw[:], N, "w3", nc.scalar.copy)
         z0_grouped = group(z_rows[0][:], PAIRS, "z0", nc.scalar.copy)
+        w3_grouped = group(w3_raw[:], N, "w3", nc.scalar.copy)
 
         y_banks = [psum.tile([P, N_TILES, P], F32, name="y_bank", tag="bank%d" % c) for c in range(PAIRS // P)]
-        spare = ["w1_raw_1_0_0", "w1_raw_1_1_0", "w1_raw_1_2_0", "w1_raw_0_0_0", "w1_raw_0_1_0", "w1_raw_0_1_1"]
 
         def w3_pass(c):
             for u in range(N_TILES):
@@ -239,7 +265,7 @@ def tile_list_carrier_mismatch_scores_kernel(
                     lhsT_scale=w3_scales[:, P * u : P * (u + 1)],
                     rhs=ride_codes[:, c * P : (c + 1) * P].bitcast(FP8X4),
                     rhs_scale=ride_scales[:, c * P : (c + 1) * P],
-                    start=(u == 0),
+                    start=False,
                     stop=False,
                 )
 
@@ -251,13 +277,13 @@ def tile_list_carrier_mismatch_scores_kernel(
                     lhsT_scale=w2_scale_t[:, b, P * u : P * (u + 1)],
                     rhs=codes[:, i * P : (i + 1) * P].bitcast(FP8X4),
                     rhs_scale=scales[:, i * P : (i + 1) * P],
-                    start=False,
+                    start=(b == 0 and u == 0),
                     stop=(b == H_PASSES - 1 and u == N_TILES - 1),
                 )
 
         def finish(j0, width, codes, scales):
-            size = tile([P, N_TILES, width], F32, "size", tag=spare.pop())
-            score = tile([P, N_TILES, width], F32, "score", tag=spare.pop())
+            size = tile([P, N_TILES, width], F32, "size_%d" % j0)
+            score = tile([P, N_TILES, width], F32, "score_%d" % j0)
             for i in range(width // P):
                 w2_pass(j0 // P + i, 1, codes, scales, i)
                 nc.scalar.activation(size[:, :, i * P : (i + 1) * P], y_banks[j0 // P + i][:], ACT.Abs)
@@ -266,17 +292,17 @@ def tile_list_carrier_mismatch_scores_kernel(
             nc.sync.dma_start(out[:, j0 : j0 + width].rearrange("(u p) j -> p u j", p=P), score[:])
 
         for t in range(PACK):
-            mismatch(1, in_two(t, 0, 256))
-        w3_codes, w3_scales = quantize(w3_grouped, N, "w3")
-        for c in range(PAIRS // P):
-            w3_pass(c)
-        za_grouped = group(z_rows[1][:, :, 0:256], 256, "za", nc.scalar.copy)
-        mismatch(1, [(0, 256, 128), (1, 256, 128)], left_tag="w3_grouped")
+            mismatch(1, in_two(t, 0, 256), on_scalar=(t < 2))
         z0_codes, z0_scales = quantize(z0_grouped, PAIRS, "z0")
-        za_codes, za_scales = quantize(za_grouped, 256, "za")
         for c in range(PAIRS // P):
             w2_pass(c, 0, z0_codes, z0_scales, c)
-        mismatch(1, [(2, 256, 128), (3, 256, 128)], left_tag="z0_grouped", diff_tag="za_grouped")
+        za_grouped = group(z_rows[1][:, :, 0:256], 256, "za", nc.scalar.copy)
+        mismatch(1, [(0, 256, 128), (1, 256, 128)], left_tag="z0_grouped")
+        w3_codes, w3_scales = quantize(w3_grouped, N, "w3")
+        za_codes, za_scales = quantize(za_grouped, 256, "za")
+        for c in range(PAIRS // P):
+            w3_pass(c)
+        mismatch(1, [(2, 256, 128), (3, 256, 128)], left_tag="w3_grouped", diff_tag="za_grouped")
         zb_grouped = group(z_rows[1][:, :, 256:384], 128, "zb", nc.scalar.copy)
         finish(0, 256, za_codes, za_scales)
         mismatch(1, [(0, 384, 128), (1, 384, 128)])

@@ -41,23 +41,19 @@ def tile_list_carrier_mismatch_scores_kernel(
 
         table_scales = tile([P, T], U8, "table_scales", tag="stage_a")
         nc.vector.memset(table_scales[0:32, :].bitcast(I32), 0)
-        nc.gpsimd.memset(table_scales[64:112, :].bitcast(I32), 0)
+        nc.vector.memset(table_scales[64:112, :].bitcast(I32), 0)
         gathered_scales = tile([P, S], U8, "gathered_scales")
         picked_scales = [tile([P, S], U8, "picked_scales%d" % a) for a in range(K_PASSES)]
         one = tile([P, 1], F32, "one")
         nc.vector.memset(one[:], 1.0)
         for a in range(K_PASSES):
-            nc.vector.memset(picked_scales[a][:].bitcast(I32), 0)
-        w2_scale_t = tile([P, H_PASSES, N], U8, "w2_scale_t")
-        nc.gpsimd.memset(w2_scale_t[:].bitcast(I32), 0)
+            nc.gpsimd.memset(picked_scales[a][:].bitcast(I32), 0)
         warm = tile([P, 1], F32, "warm")
         nc.scalar.activation(warm[:], one[:], ACT.Sqrt)
 
         offs_t = tile([P, S // LIST_COL], U16, "offs_t")
         pos1_t = tile([P, PAIRS // LIST_COL], U16, "pos1_t")
         pos2_t = tile([P, PAIRS // LIST_COL], U16, "pos2_t")
-        gain_t = [tile([P, PACK], F32, "gain_t%d" % b) for b in range(H_PASSES)]
-        base_t = tile([P, N_TILES], F32, "base_t")
         table_words, w1_raw = {}, {}
 
         def load_words(a, stage):
@@ -83,18 +79,7 @@ def tile_list_carrier_mismatch_scores_kernel(
         nc.sync.dma_start(pos2_t[:], pos2)
         load_words(1, "stage_c")
         load_w1(0, 0, 0, "stage_d")
-        with nc.allow_non_contiguous_dma(reason="one value a partition"):
-            nc.gpsimd.dma_start(gain_t[0][:], gain[0:K_PASS].rearrange("(m p) -> p m", p=P))
-        nc.gpsimd.dma_start(gain_t[1][:], gain[K_PASS:H].rearrange("(p t) -> p t", t=PACK))
-        w2_word_t = tile([P, H_PASSES, 2 * N], U8, "w2_word_t")
-        nc.gpsimd.dma_start(w2_word_t[:].bitcast(I32), w2_words.rearrange("a p n -> p a n").bitcast(I32))
-        for q in range(4):
-            nc.gpsimd.dma_start(
-                w2_scale_t[32 * q : 32 * q + 4].bitcast(I32),
-                w2_scales[:, 4 * q : 4 * q + 4, :].rearrange("a r n -> r a n").bitcast(I32),
-            )
-        with nc.allow_non_contiguous_dma(reason="one value a partition"):
-            nc.gpsimd.dma_start(base_t[:], base.rearrange("(u p) -> p u", p=P))
+        load_w1(0, 1, 0, "stage_e")
 
         picked_words = [tile([P, S], U16, "picked_words%d" % a) for a in range(K_PASSES)]
         w1_grouped, w1_mx = {}, {}
@@ -134,8 +119,8 @@ def tile_list_carrier_mismatch_scores_kernel(
             else:
                 grouped = tile([P, K_PASS, PACK], BF16, name + "_grouped", tag=name + "_grouped")
                 nc.scalar.copy(
-                    grouped[:].rearrange("p (t m) j -> p m j t", t=PACK),
-                    w1_raw[b, a, part][:].rearrange("p j (m t) -> p m j t", t=PACK),
+                    grouped[:].rearrange("p (t m e) j -> p m j e t", t=PACK, e=2),
+                    w1_raw[b, a, part][:].rearrange("p j (m e t) -> p m j e t", t=PACK, e=2),
                 )
                 w1_grouped[b, a, part] = grouped
 
@@ -145,25 +130,32 @@ def tile_list_carrier_mismatch_scores_kernel(
 
         nc.vector.tensor_copy(gathered_scales[:], table_scales[:].indirect(offs_t[:]))
         place_scales(0)
-        load_w1(0, 1, 0, "stage_a")
+        load_words(2, "stage_a")
         place_scales(1)
         gather_words(0)
-        load_words(2, "stage_b")
-        group_w1(0, 0, 0)
-        load_w1(0, 2, 0, "stage_d")
+        load_w1(0, 2, 0, "stage_b")
         place_scales(2)
+        group_w1(0, 0, 0)
+        load_w1(0, 0, 1, "stage_d")
         gather_words(1)
-        load_w1(0, 0, 1, "stage_c")
+        load_w1(0, 1, 1, "stage_c")
         quantize_w1(0, 0, 0)
         group_w1(0, 1, 0)
-        load_w1(0, 1, 1, "stage_a")
+        load_w1(0, 2, 1, "stage_e")
         quantize_w1(0, 1, 0)
+        gain_t = [tile([P, PACK], F32, "gain_t", tag="w1_0_%d_0_grouped" % b) for b in range(H_PASSES)]
+        with nc.allow_non_contiguous_dma(reason="one value a partition"):
+            nc.sync.dma_start(gain_t[0][:], gain[0:K_PASS].rearrange("(m p) -> p m", p=P))
+        nc.sync.dma_start(gain_t[1][:], gain[K_PASS:H].rearrange("(p t) -> p t", t=PACK))
         gather_words(2)
-        load_w1(0, 2, 1, "stage_b")
-        group_w1(0, 2, 0)
-        load_w1(1, 0, 0, "stage_d")
-        quantize_w1(0, 2, 0)
-        load_w1(1, 1, 0, "w1_0_2_0_grouped")
+        load_w1(1, 0, 0, "stage_a")
+        last_raw = w1_raw[0, 2, 0]
+        last_grouped = [
+            group(last_raw[:, :, m * P : (m + 1) * P], P, "w1_last%d" % m, copy)
+            for m, copy in enumerate((nc.vector.tensor_copy, nc.scalar.copy))
+        ]
+        load_w1(1, 1, 0, "stage_b")
+        last_mx = [quantize(last_grouped[m], P, "w1_last%d" % m) for m in range(2)]
 
         halves = [slice(i * BANK, (i + 1) * BANK) for i in range(S // BANK)]
         h_rows = {}
@@ -174,9 +166,12 @@ def tile_list_carrier_mismatch_scores_kernel(
                 for i in range(2):
                     banks[t, i] = psum.tile([P, BANK], F32, name="h_bank", tag="bank%d" % (2 * t + i))
             for a in range(K_PASSES):
-                codes, scales = w1_mx[b, a, part]
                 for t in slices:
-                    cols = slice((t - slices[0]) * P, (t - slices[0] + 1) * P)
+                    if (b, a, part) == (0, 2, 0):
+                        (codes, scales), cols = last_mx[t], slice(0, P)
+                    else:
+                        codes, scales = w1_mx[b, a, part]
+                        cols = slice((t - slices[0]) * P, (t - slices[0] + 1) * P)
                     for i, js in enumerate(halves):
                         nc.tensor.matmul_mx(
                             out=banks[t, i][:],
@@ -229,23 +224,35 @@ def tile_list_carrier_mismatch_scores_kernel(
 
         features(0, 0, [0, 1])
         part = K_PASS // 2
-        late_a = tile([P, part, PACK], BF16, "late_a", tag="w1_0_2_0_codes")
-        late_b = tile([P, 2 * part, PACK], BF16, "late_b", tag="w1_0_2_0_scales")
+        late_a = tile([P, part, PACK], BF16, "late_a", tag="w1_last1_codes")
+        late_b = tile([P, 2 * part, PACK], BF16, "late_b", tag="w1_last1_scales")
         group(w1_raw[0, 0, 1][:], part, "", nc.scalar.copy, late_a)
-        load_w1(1, 2, 0, "stage_c")
+        load_w1(1, 2, 0, "stage_d")
         group(w1_raw[0, 1, 1][:], part, "", nc.scalar.copy, late_b[:, 0:part, :])
-        ride_raw = load_rows(ride, "stage_a")
+        ride_raw = load_rows(ride, "stage_c")
         group(w1_raw[0, 2, 1][:], part, "", nc.scalar.copy, late_b[:, part : 2 * part, :])
-        w3_raw = load_rows(w3, "stage_b")
+        w3_raw = load_rows(w3, "stage_e")
         first_half_slice(0)
         w1_mx[0, 0, 1] = quantize(late_a, part, "late_a")
         codes, scales = quantize(late_b, 2 * part, "late_b")
         for a in (1, 2):
             w1_mx[0, a, 1] = codes[:, (a - 1) * part : a * part], scales[:, (a - 1) * part : a * part]
         features(0, 1, [2, 3])
+        w2_scale_t = tile([P, H_PASSES, N], U8, "w2_scale_t", tag="late_a_codes")
+        nc.gpsimd.memset(w2_scale_t[:].bitcast(I32), 0)
+        for q in range(4):
+            nc.sync.dma_start(
+                w2_scale_t[32 * q : 32 * q + 4].bitcast(I32),
+                w2_scales[:, 4 * q : 4 * q + 4, :].rearrange("a r n -> r a n").bitcast(I32),
+            )
+        w2_word_t = tile([P, H_PASSES, 2 * N], U8, "w2_word_t", tag="late_b_codes")
+        nc.sync.dma_start(w2_word_t[:].bitcast(I32), w2_words.rearrange("a p n -> p a n").bitcast(I32))
+        base_t = tile([P, N_TILES], F32, "base_t", tag="late_b_scales")
+        with nc.allow_non_contiguous_dma(reason="one value a partition"):
+            nc.sync.dma_start(base_t[:], base.rearrange("(u p) -> p u", p=P))
         for a in range(K_PASSES):
             group_w1(1, a, 0)
-        first_half_slice(1, left_tag="w1_0_2_0_codes", diff_tag="w1_0_2_0_scales")
+        first_half_slice(1, left_tag="w1_last1_codes", diff_tag="w1_last1_scales")
         first_half_slice(2)
         for a in range(K_PASSES):
             quantize_w1(1, a, 0)
@@ -292,7 +299,7 @@ def tile_list_carrier_mismatch_scores_kernel(
             nc.sync.dma_start(out[:, j0 : j0 + width].rearrange("(u p) j -> p u j", p=P), score[:])
 
         for t in range(PACK):
-            mismatch(1, in_two(t, 0, 256), on_scalar=(t < 2))
+            mismatch(1, in_two(t, 0, 256))
         z0_codes, z0_scales = quantize(z0_grouped, PAIRS, "z0")
         for c in range(PAIRS // P):
             w2_pass(c, 0, z0_codes, z0_scales, c)

@@ -185,7 +185,7 @@ def tile_list_carrier_mismatch_scores_kernel(
             for t in slices:
                 h_rows[b, t] = tile([P, S], F32, "h_%d_%d" % (b, t))
                 for i, js in enumerate(halves):
-                    copy = nc.vector.tensor_copy if (b, t, i) == (0, 0, 1) else nc.scalar.copy
+                    copy = nc.vector.tensor_copy if (b, t, i) in ((0, 0, 1), (0, 2, 1)) else nc.scalar.copy
                     copy(h_rows[b, t][:, js], banks[t, i][:])
 
         z_rows = [tile([P, PACK, PAIRS], BF16, "z_rows%d" % b) for b in range(H_PASSES)]
@@ -262,12 +262,20 @@ def tile_list_carrier_mismatch_scores_kernel(
         z0_grouped = group(z_rows[0][:], PAIRS, "z0", nc.scalar.copy)
         w3_grouped = group(w3_raw[:], N, "w3", nc.scalar.copy)
 
-        y_banks = [psum.tile([P, N_TILES, P], F32, name="y_bank", tag="bank%d" % c) for c in range(PAIRS // P)]
+        chunks = PAIRS // P
+        y_banks = [psum.tile([P, N_TILES, P], F32, name="y_bank", tag="bank%d" % c) for c in range(chunks - 1)]
+        last_banks = [psum.tile([P, 2, P], F32, name="y_last", tag="bank%d" % (chunks - 1 + i)) for i in range(2)]
+
+        def y_part(c, u):
+            if c < chunks - 1:
+                return y_banks[c][:, u, :], u == 0, u == N_TILES - 1
+            return last_banks[u // 2][:, u % 2, :], u % 2 == 0, u % 2 == 1
 
         def w3_pass(c):
             for u in range(N_TILES):
+                part, first, last = y_part(c, u)
                 nc.tensor.matmul_mx(
-                    out=y_banks[c][:, u, :],
+                    out=part,
                     lhsT=w3_codes[:, P * u : P * (u + 1)].bitcast(FP8X4),
                     lhsT_scale=w3_scales[:, P * u : P * (u + 1)],
                     rhs=ride_codes[:, c * P : (c + 1) * P].bitcast(FP8X4),
@@ -278,15 +286,18 @@ def tile_list_carrier_mismatch_scores_kernel(
 
         def w2_pass(c, b, codes, scales, i):
             for u in range(N_TILES):
+                part, first, last = y_part(c, u)
                 nc.tensor.matmul_mx(
-                    out=y_banks[c][:, u, :],
+                    out=part,
                     lhsT=w2_word_t[:, b, 2 * P * u : 2 * P * (u + 1)].bitcast(FP4X4),
                     lhsT_scale=w2_scale_t[:, b, P * u : P * (u + 1)],
                     rhs=codes[:, i * P : (i + 1) * P].bitcast(FP8X4),
                     rhs_scale=scales[:, i * P : (i + 1) * P],
-                    start=(b == 0 and u == 0),
-                    stop=(b == H_PASSES - 1 and u == N_TILES - 1),
+                    start=(b == 0 and first),
+                    stop=(b == H_PASSES - 1 and last),
                 )
+
+        out_tiles = out.rearrange("(u p) j -> p u j", p=P)
 
         def finish(j0, width, codes, scales):
             size = tile([P, N_TILES, width], F32, "size_%d" % j0)
@@ -296,25 +307,42 @@ def tile_list_carrier_mismatch_scores_kernel(
                 nc.scalar.activation(size[:, :, i * P : (i + 1) * P], y_banks[j0 // P + i][:], ACT.Abs)
             for u in range(N_TILES):
                 nc.scalar.activation(score[:, u, :], size[:, u, :], ACT.Sqrt, bias=base_t[:, u : u + 1])
-            nc.sync.dma_start(out[:, j0 : j0 + width].rearrange("(u p) j -> p u j", p=P), score[:])
+            nc.sync.dma_start(out_tiles[:, :, j0 : j0 + width], score[:])
+
+        def finish_last(codes, scales):
+            j0 = PAIRS - P
+            w2_pass(chunks - 1, 1, codes, scales, 0)
+            negated = tile([P, 2, P], F32, "negated")
+            size = [tile([P, 2, P], F32, "size_last%d" % i) for i in range(2)]
+            nc.vector.tensor_scalar(negated[:], last_banks[0][:], -1.0, None, ALU.mult)
+            nc.vector.tensor_tensor(size[0][:], last_banks[0][:], negated[:], ALU.max)
+            nc.scalar.activation(size[1][:], last_banks[1][:], ACT.Abs)
+            for i in (1, 0):
+                score = tile([P, 2, P], F32, "score_last%d" % i)
+                for e in range(2):
+                    u = 2 * i + e
+                    nc.scalar.activation(score[:, e, :], size[i][:, e, :], ACT.Sqrt, bias=base_t[:, u : u + 1])
+                nc.sync.dma_start(out_tiles[:, 2 * i : 2 * i + 2, j0:PAIRS], score[:])
 
         for t in range(PACK):
-            mismatch(1, in_two(t, 0, 256))
+            mismatch(1, in_two(t, 0, 256), on_scalar=(t < 1))
         z0_codes, z0_scales = quantize(z0_grouped, PAIRS, "z0")
-        for c in range(PAIRS // P):
+        for c in range(chunks):
             w2_pass(c, 0, z0_codes, z0_scales, c)
         za_grouped = group(z_rows[1][:, :, 0:256], 256, "za", nc.scalar.copy)
         mismatch(1, [(0, 256, 128), (1, 256, 128)], left_tag="z0_grouped")
         w3_codes, w3_scales = quantize(w3_grouped, N, "w3")
         za_codes, za_scales = quantize(za_grouped, 256, "za")
-        for c in range(PAIRS // P):
+        for c in (0, 1):
             w3_pass(c)
         mismatch(1, [(2, 256, 128), (3, 256, 128)], left_tag="w3_grouped", diff_tag="za_grouped")
-        zb_grouped = group(z_rows[1][:, :, 256:384], 128, "zb", nc.scalar.copy)
         finish(0, 256, za_codes, za_scales)
-        mismatch(1, [(0, 384, 128), (1, 384, 128)])
+        for c in (2, 3):
+            w3_pass(c)
+        zb_grouped = group(z_rows[1][:, :, 256:384], 128, "zb", nc.vector.tensor_copy)
         zb_codes, zb_scales = quantize(zb_grouped, 128, "zb")
-        mismatch(1, [(2, 384, 128), (3, 384, 128)], left_tag="zb_grouped")
+        mismatch(1, [(0, 384, 128), (1, 384, 128)], diff_tag="zb_grouped")
+        mismatch(1, [(2, 384, 128), (3, 384, 128)])
         finish(256, 128, zb_codes, zb_scales)
         zc_codes, zc_scales = quantize(group(z_rows[1][:, :, 384:512], 128, "zc", nc.vector.tensor_copy), 128, "zc")
-        finish(384, 128, zc_codes, zc_scales)
+        finish_last(zc_codes, zc_scales)

from contextlib import ExitStack

import concourse.mybir as mybir

K, T, S, PAIRS, H, M, N = 1536, 4096, 1024, 512, 1024, 512, 512
FLOPS = 2 * K * H * S + 2 * H * N * PAIRS + 2 * M * N * PAIRS

F32 = mybir.dt.float32
BF16 = mybir.dt.bfloat16
I32 = mybir.dt.int32
U32 = mybir.dt.uint32
U16 = mybir.dt.uint16
U8 = mybir.dt.uint8
FP8X4 = mybir.dt.float8_e4m3fn_x4
FP4X4 = mybir.dt.float4_e2m1fn_x4
ALU = mybir.AluOpType
ACT = mybir.ActivationFunctionType

P = 128
PACK = 4
K_PASS = P * PACK
BANK = 512
K_PASSES = K // K_PASS
H_PASSES = H // K_PASS
N_TILES = N // P
LIST_COL = 16
SCALE_ROW = (32, 48, 112)
LAST_CHUNKS = (256, 128, 128)


def tile_list_carrier_mismatch_scores_kernel(
    tc, tab_words, tab_scales, offs, pos1, pos2, w1, gain, w2_words, w2_scales, ride, w3, base, out
):
    nc = tc.nc
    with ExitStack() as ctx:
        held = ctx.enter_context(tc.tile_pool(name="held", bufs=1))
        psum = ctx.enter_context(tc.psum_pool(name="psum", bufs=1))

        def tile(shape, dtype, name, **kw):
            return held.tile(shape, dtype, name=name, align_bytes=64, **kw)

        table_scales = tile([P, T], U8, "table_scales", tag="stage_a")
        nc.vector.memset(table_scales[0:32, :].bitcast(I32), 0)
        nc.vector.memset(table_scales[64:112, :].bitcast(I32), 0)
        gathered_scales = tile([P, S], U8, "gathered_scales")
        picked_scales = [tile([P, S], U8, "picked_scales%d" % a) for a in range(K_PASSES)]
        one = tile([P, 1], F32, "one")
        nc.vector.memset(one[:], 1.0)
        for a in range(K_PASSES):
            nc.gpsimd.memset(picked_scales[a][:].bitcast(I32), 0)
        warm = tile([P, 1], F32, "warm")
        nc.scalar.activation(warm[:], one[:], ACT.Sqrt)

        offs_t = tile([P, S // LIST_COL], U16, "offs_t")
        pos1_t = tile([P, PAIRS // LIST_COL], U16, "pos1_t")
        pos2_t = tile([P, PAIRS // LIST_COL], U16, "pos2_t")
        table_words, w1_raw = {}, {}

        def load_words(a, stage):
            table_words[a] = tile([P, T], U16, "table_words", tag=stage)
            nc.sync.dma_start(table_words[a][:].bitcast(I32), tab_words[a].bitcast(I32))

        def load_rows(rows, stage):
            raw = tile([P, PACK, rows.shape[1]], F32, "raw", tag=stage)
            nc.sync.dma_start(raw[:], rows.rearrange("(p j) c -> p j c", j=PACK))
            return raw

        def load_w1(b, a, part, stage):
            width = K_PASS // 2 if b == 0 else K_PASS
            c0 = b * K_PASS + part * width
            w1_raw[b, a, part] = load_rows(w1[a * K_PASS : (a + 1) * K_PASS, c0 : c0 + width], stage)

        scale_rows = tab_scales.rearrange("a q t -> (a q) t")
        nc.sync.dma_start(offs_t[:], offs)
        nc.sync.dma_start(table_scales[32:64, :].bitcast(I32), scale_rows[0:32, :].bitcast(I32))
        nc.sync.dma_start(table_scales[112:128, :].bitcast(I32), scale_rows[32:48, :].bitcast(I32))
        load_words(0, "stage_b")
        nc.sync.dma_start(pos1_t[:], pos1)
        nc.sync.dma_start(pos2_t[:], pos2)
        load_words(1, "stage_c")
        load_w1(0, 0, 0, "stage_d")
        load_w1(0, 1, 0, "stage_e")

        picked_words = [tile([P, S], U16, "picked_words%d" % a) for a in range(K_PASSES)]
        w1_grouped, w1_mx = {}, {}

        def gather_words(a):
            nc.vector.tensor_copy(picked_words[a][:], table_words[a][:].indirect(offs_t[:]))

        def place_scales(a):
            first = SCALE_ROW[a]
            for q in range(4):
                nc.sync.dma_start(
                    picked_scales[a][32 * q : 32 * q + 4, :].bitcast(I32),
                    gathered_scales[first + 4 * q : first + 4 * q + 4, :].bitcast(I32),
                )

        def group(rows, width, name, engine_copy, grouped=None):
            if grouped is None:
                grouped = tile([P, width, PACK], BF16, name + "_grouped", tag=name + "_grouped")
            engine_copy(
                grouped[:].rearrange("p (c i) t -> p c t i", i=PACK),
                rows.rearrange("p t (c i) -> p c t i", i=PACK),
            )
            return grouped

        def quantize(grouped, width, name):
            codes = tile([P, width], U32, name + "_codes", tag=name + "_codes")
            scales = tile([P, width], U8, name + "_scales", tag=name + "_scales")
            nc.vector.quantize_mx(
                out=codes[:].bitcast(FP8X4), scales=scales[:], in_=grouped[:].rearrange("p c t -> p (c t)")
            )
            return codes, scales

        def group_w1(b, a, part):
            name = "w1_%d_%d_%d" % (b, a, part)
            if b == 0:
                w1_grouped[b, a, part] = group(w1_raw[b, a, part][:], K_PASS // 2, name, nc.scalar.copy)
            else:
                grouped = tile([P, K_PASS, PACK], BF16, name + "_grouped", tag=name + "_grouped")
                nc.scalar.copy(
                    grouped[:].rearrange("p (t m e) j -> p m j e t", t=PACK, e=2),
                    w1_raw[b, a, part][:].rearrange("p j (m e t) -> p m j e t", t=PACK, e=2),
                )
                w1_grouped[b, a, part] = grouped

        def quantize_w1(b, a, part):
            grouped = w1_grouped[b, a, part]
            w1_mx[b, a, part] = quantize(grouped, grouped.shape[1], "w1_%d_%d_%d" % (b, a, part))

        nc.vector.tensor_copy(gathered_scales[:], table_scales[:].indirect(offs_t[:]))
        place_scales(0)
        load_words(2, "stage_a")
        place_scales(1)
        gather_words(0)
        load_w1(0, 2, 0, "stage_b")
        place_scales(2)
        group_w1(0, 0, 0)
        load_w1(0, 0, 1, "stage_d")
        gather_words(1)
        load_w1(0, 1, 1, "stage_c")
        quantize_w1(0, 0, 0)
        group_w1(0, 1, 0)
        load_w1(0, 2, 1, "stage_e")
        quantize_w1(0, 1, 0)
        gain_t = [tile([P, PACK], F32, "gain_t", tag="w1_0_%d_0_grouped" % b) for b in range(H_PASSES)]
        with nc.allow_non_contiguous_dma(reason="one value a partition"):
            nc.sync.dma_start(gain_t[0][:], gain[0:K_PASS].rearrange("(m p) -> p m", p=P))
        nc.sync.dma_start(gain_t[1][:], gain[K_PASS:H].rearrange("(p t) -> p t", t=PACK))
        gather_words(2)
        load_w1(1, 0, 0, "stage_a")
        last_raw = w1_raw[0, 2, 0]
        last_grouped = [
            group(last_raw[:, :, m * P : (m + 1) * P], P, "w1_last%d" % m, copy)
            for m, copy in enumerate((nc.vector.tensor_copy, nc.scalar.copy))
        ]
        load_w1(1, 1, 0, "stage_b")
        last_mx = [quantize(last_grouped[m], P, "w1_last%d" % m) for m in range(2)]

        halves = [slice(i * BANK, (i + 1) * BANK) for i in range(S // BANK)]
        h_rows = {}

        def features(b, part, slices):
            banks = {}
            for t in slices:
                for i in range(2):
                    banks[t, i] = psum.tile([P, BANK], F32, name="h_bank", tag="bank%d" % (2 * t + i))
            for a in range(K_PASSES):
                for t in slices:
                    if (b, a, part) == (0, 2, 0):
                        (codes, scales), cols = last_mx[t], slice(0, P)
                    else:
                        codes, scales = w1_mx[b, a, part]
                        cols = slice((t - slices[0]) * P, (t - slices[0] + 1) * P)
                    for i, js in enumerate(halves):
                        nc.tensor.matmul_mx(
                            out=banks[t, i][:],
                            lhsT=codes[:, cols].bitcast(FP8X4),
                            lhsT_scale=scales[:, cols],
                            rhs=picked_words[a][:, js].bitcast(FP4X4),
                            rhs_scale=picked_scales[a][:, js],
                            start=(a == 0),
                            stop=(a == K_PASSES - 1),
                        )
            for t in slices:
                h_rows[b, t] = tile([P, S], F32, "h_%d_%d" % (b, t))
                for i, js in enumerate(halves):
                    copy = nc.vector.tensor_copy if (b, t, i) in ((0, 0, 1), (0, 2, 1)) else nc.scalar.copy
                    copy(h_rows[b, t][:, js], banks[t, i][:])

        z_rows = [tile([P, PACK, PAIRS], BF16, "z_rows%d" % b) for b in range(H_PASSES)]
        z_plain = [tile([P, PAIRS], BF16, "z_plain%d" % m) for m in range(PACK)]

        def mismatch(b, units, left_tag=None, diff_tag=None, on_scalar=False):
            width = units[0][2]
            shape = [P, len(units), width]
            left = tile(shape, F32, "left", tag=left_tag) if left_tag else tile(shape, F32, "left", tag="left", bufs=2)
            diff = tile(shape, F32, "diff", tag=diff_tag) if diff_tag else tile(shape, F32, "diff", tag="diff", bufs=4)
            lists = [slice(j0 // LIST_COL, (j0 + width) // LIST_COL) for t, j0, w in units]
            for i, (t, j0, w) in enumerate(units):
                nc.vector.tensor_copy(left[:, i, :], h_rows[b, t][:].indirect(pos1_t[:, lists[i]]))
            for i, (t, j0, w) in enumerate(units):
                nc.vector.tensor_tensor(
                    diff[:, i, :], h_rows[b, t][:].indirect(pos2_t[:, lists[i]]), left[:, i, :], ALU.subtract
                )
            if on_scalar:
                t, j0 = units[0][0], units[0][1]
                js = slice(j0, j0 + len(units) * width)
                z = z_plain[t][:, js] if b == 0 else z_rows[b][:, t, js]
                flat = diff[:].rearrange("p i w -> p (i w)")
                nc.scalar.activation(flat, flat, ACT.Square)
                nc.scalar.activation(z, flat, ACT.Copy, scale=gain_t[b][:, t : t + 1])
                return
            for i, (t, j0, w) in enumerate(units):
                z = z_plain[t][:, j0 : j0 + width] if b == 0 else z_rows[b][:, t, j0 : j0 + width]
                nc.vector.scalar_tensor_tensor(z, diff[:, i, :], gain_t[b][:, t : t + 1], diff[:, i, :], ALU.mult, ALU.mult)

        def in_two(t, j0, width):
            return [(t, j0, width // 2), (t, j0 + width // 2, width // 2)]

        def first_half_slice(m, **holds):
            mismatch(0, in_two(m, 0, PAIRS), **holds)
            nc.sync.dma_start(z_rows[0][32 * m : 32 * (m + 1)], z_plain[m][:])

        features(0, 0, [0, 1])
        part = K_PASS // 2
        late_a = tile([P, part, PACK], BF16, "late_a", tag="w1_last1_codes")
        late_b = tile([P, 2 * part, PACK], BF16, "late_b", tag="w1_last1_scales")
        group(w1_raw[0, 0, 1][:], part, "", nc.scalar.copy, late_a)
        load_w1(1, 2, 0, "stage_d")
        group(w1_raw[0, 1, 1][:], part, "", nc.scalar.copy, late_b[:, 0:part, :])
        ride_raw = load_rows(ride, "stage_c")
        group(w1_raw[0, 2, 1][:], part, "", nc.scalar.copy, late_b[:, part : 2 * part, :])
        w3_raw = load_rows(w3, "stage_e")
        first_half_slice(0)
        w1_mx[0, 0, 1] = quantize(late_a, part, "late_a")
        codes, scales = quantize(late_b, 2 * part, "late_b")
        for a in (1, 2):
            w1_mx[0, a, 1] = codes[:, (a - 1) * part : a * part], scales[:, (a - 1) * part : a * part]
        features(0, 1, [2, 3])
        w2_scale_t = tile([P, H_PASSES, N], U8, "w2_scale_t", tag="late_a_codes")
        nc.gpsimd.memset(w2_scale_t[:].bitcast(I32), 0)
        for q in range(4):
            nc.sync.dma_start(
                w2_scale_t[32 * q : 32 * q + 4].bitcast(I32),
                w2_scales[:, 4 * q : 4 * q + 4, :].rearrange("a r n -> r a n").bitcast(I32),
            )
        w2_word_t = tile([P, H_PASSES, 2 * N], U8, "w2_word_t", tag="late_b_codes")
        nc.sync.dma_start(w2_word_t[:].bitcast(I32), w2_words.rearrange("a p n -> p a n").bitcast(I32))
        base_t = tile([P, N_TILES], F32, "base_t", tag="late_b_scales")
        with nc.allow_non_contiguous_dma(reason="one value a partition"):
            nc.sync.dma_start(base_t[:], base.rearrange("(u p) -> p u", p=P))
        for a in range(K_PASSES):
            group_w1(1, a, 0)
        first_half_slice(1, left_tag="w1_last1_codes", diff_tag="w1_last1_scales")
        first_half_slice(2)
        for a in range(K_PASSES):
            quantize_w1(1, a, 0)
        features(1, 0, [0, 1, 2, 3])
        first_half_slice(3, left_tag="w1_1_1_0_grouped", diff_tag="w1_1_2_0_grouped")
        ride_codes, ride_scales = quantize(group(ride_raw[:], PAIRS, "ride", nc.scalar.copy), PAIRS, "ride")
        z0_grouped = group(z_rows[0][:], PAIRS, "z0", nc.scalar.copy)
        w3_grouped = group(w3_raw[:], N, "w3", nc.scalar.copy)

        chunks = PAIRS // P
        y_banks = [psum.tile([P, N_TILES, P], F32, name="y_bank", tag="bank%d" % c) for c in range(chunks - 1)]
        last_banks = [psum.tile([P, 2, P], F32, name="y_last", tag="bank%d" % (chunks - 1 + i)) for i in range(2)]

        def y_part(c, u):
            if c < chunks - 1:
                return y_banks[c][:, u, :], u == 0, u == N_TILES - 1
            return last_banks[u // 2][:, u % 2, :], u % 2 == 0, u % 2 == 1

        def w3_pass(c):
            for u in range(N_TILES):
                part, first, last = y_part(c, u)
                nc.tensor.matmul_mx(
                    out=part,
                    lhsT=w3_codes[:, P * u : P * (u + 1)].bitcast(FP8X4),
                    lhsT_scale=w3_scales[:, P * u : P * (u + 1)],
                    rhs=ride_codes[:, c * P : (c + 1) * P].bitcast(FP8X4),
                    rhs_scale=ride_scales[:, c * P : (c + 1) * P],
                    start=False,
                    stop=False,
                )

        def w2_pass(c, b, codes, scales, i):
            for u in range(N_TILES):
                part, first, last = y_part(c, u)
                nc.tensor.matmul_mx(
                    out=part,
                    lhsT=w2_word_t[:, b, 2 * P * u : 2 * P * (u + 1)].bitcast(FP4X4),
                    lhsT_scale=w2_scale_t[:, b, P * u : P * (u + 1)],
                    rhs=codes[:, i * P : (i + 1) * P].bitcast(FP8X4),
                    rhs_scale=scales[:, i * P : (i + 1) * P],
                    start=(b == 0 and first),
                    stop=(b == H_PASSES - 1 and last),
                )

        out_tiles = out.rearrange("(u p) j -> p u j", p=P)

        def finish(j0, width, codes, scales):
            size = tile([P, N_TILES, width], F32, "size_%d" % j0)
            score = tile([P, N_TILES, width], F32, "score_%d" % j0)
            for i in range(width // P):
                w2_pass(j0 // P + i, 1, codes, scales, i)
                nc.scalar.activation(size[:, :, i * P : (i + 1) * P], y_banks[j0 // P + i][:], ACT.Abs)
            for u in range(N_TILES):
                nc.scalar.activation(score[:, u, :], size[:, u, :], ACT.Sqrt, bias=base_t[:, u : u + 1])
            nc.sync.dma_start(out_tiles[:, :, j0 : j0 + width], score[:])

        def finish_last(codes, scales):
            j0 = PAIRS - P
            w2_pass(chunks - 1, 1, codes, scales, 0)
            negated = tile([P, 2, P], F32, "negated")
            size = [tile([P, 2, P], F32, "size_last%d" % i) for i in range(2)]
            nc.vector.tensor_scalar(negated[:], last_banks[0][:], -1.0, None, ALU.mult)
            nc.vector.tensor_tensor(size[0][:], last_banks[0][:], negated[:], ALU.max)
            nc.scalar.activation(size[1][:], last_banks[1][:], ACT.Abs)
            for i in (1, 0):
                score = tile([P, 2, P], F32, "score_last%d" % i)
                for e in range(2):
                    u = 2 * i + e
                    nc.scalar.activation(score[:, e, :], size[i][:, e, :], ACT.Sqrt, bias=base_t[:, u : u + 1])
                nc.sync.dma_start(out_tiles[:, 2 * i : 2 * i + 2, j0:PAIRS], score[:])

        for t in range(PACK):
            mismatch(1, in_two(t, 0, 256), on_scalar=(t < 1))
        z0_codes, z0_scales = quantize(z0_grouped, PAIRS, "z0")
        for c in range(chunks):
            w2_pass(c, 0, z0_codes, z0_scales, c)
        za_grouped = group(z_rows[1][:, :, 0:256], 256, "za", nc.scalar.copy)
        mismatch(1, [(0, 256, 128), (1, 256, 128)], left_tag="z0_grouped")
        w3_codes, w3_scales = quantize(w3_grouped, N, "w3")
        za_codes, za_scales = quantize(za_grouped, 256, "za")
        for c in (0, 1):
            w3_pass(c)
        mismatch(1, [(2, 256, 128), (3, 256, 128)], left_tag="w3_grouped", diff_tag="za_grouped")
        finish(0, 256, za_codes, za_scales)
        for c in (2, 3):
            w3_pass(c)
        zb_grouped = group(z_rows[1][:, :, 256:384], 128, "zb", nc.vector.tensor_copy)
        zb_codes, zb_scales = quantize(zb_grouped, 128, "zb")
        mismatch(1, [(0, 384, 128), (1, 384, 128)], diff_tag="zb_grouped")
        mismatch(1, [(2, 384, 128), (3, 384, 128)])
        finish(256, 128, zb_codes, zb_scales)
        zc_codes, zc_scales = quantize(group(z_rows[1][:, :, 384:512], 128, "zc", nc.vector.tensor_copy), 128, "zc")
        finish_last(zc_codes, zc_scales)
